import numpy as np
import ml_dtypes


def mxq(x, axis, fmt="e4m3"):
    dtype, down = {"e4m3": (ml_dtypes.float8_e4m3fn, 7), "e5m2": (ml_dtypes.float8_e5m2, 14)}[fmt]
    v = np.moveaxis(np.asarray(x, np.float32).astype(ml_dtypes.bfloat16).astype(np.float64), axis, -1)
    blocks = v.reshape(v.shape[:-1] + (-1, 32))
    amax = np.abs(blocks).max(-1, keepdims=True)
    byte = np.maximum(np.where(amax > 0, np.frexp(amax)[1] - 1 + 127, 0) - down, 1)
    scale = np.exp2(byte - 127.0)
    codes = (blocks / scale).astype(np.float32).astype(dtype).astype(np.float64)
    return np.moveaxis((codes * scale).reshape(v.shape), -1, axis)


WIDE = False


def mx_kscale(k):
    if not WIDE:
        return np.ones(k)
    levels = np.array([10, -10, 5, -5, 0])
    if k % 512:
        return np.exp2(np.random.permutation(np.resize(levels, k // 32))).repeat(32)
    a = np.empty((k // 512, 16))
    for p in range(k // 512):
        a[p, :8] = np.random.permutation(np.resize(levels, 8))
        for g in range(8):
            far = levels[np.abs(levels - a[p, g]) >= 10]
            a[p, g + 8] = far[np.random.randint(len(far))]
    return np.exp2(a.ravel()).repeat(32)


def f64(x):
    return np.asarray(x).astype(np.float64)


def striped(idx):
    return np.tile(idx.reshape(-1, 16).T, (8, 1)).astype(np.uint16)


def unstriped(offs):
    return offs[:16].T.reshape(-1).astype(np.int64)


def pack_weight(w):
    k, n = w.shape
    w = f64(np.asarray(w, np.float32).astype(ml_dtypes.bfloat16)).reshape(k // 32, 32, n)
    amax = np.abs(w).max(1)
    byte = np.clip(np.where(amax > 0, np.frexp(amax)[1] - 1 + 127 - 7, 1), 1, 254)
    scaled = (w * np.exp2(127.0 - byte)[:, None, :]).reshape(k, n).astype(np.float32)
    words = np.ascontiguousarray(scaled.reshape(k // 512, 128, 4, n).transpose(0, 1, 3, 2)).astype(ml_dtypes.float8_e4m3fn).view(np.uint8)
    return words, np.ascontiguousarray(byte.astype(np.uint8).reshape(k // 512, 16, n))


def unpack_weight(words, scales):
    g, p, n, _ = words.shape
    vals = np.ascontiguousarray(words).view(ml_dtypes.float8_e4m3fn).astype(np.float64) * np.repeat(np.exp2(scales.astype(np.float64) - 127.0), 8, axis=1)[..., None]
    return vals.transpose(0, 1, 3, 2).reshape(g * 512, n)


def sigmoid(v):
    return 1.0 / (1.0 + np.exp(-np.maximum(v, -700.0)))


K, T, S, D, N, V = 512, 4096, 1024, 8, 128, 128
P = 2 ** 7


def setup_inputs():
    n = np.random.standard_normal
    s = mx_kscale(K)[:, None]
    packed_xT = pack_weight(n((K, T)) * s)
    return {
        "x_words": packed_xT[0],
        "x_scales": packed_xT[1],
        "w1": (n((K, N)) / np.sqrt(K) / s).astype(np.float32),
        "w2": (n((K, N)) / np.sqrt(K) / s).astype(np.float32),
        "mult": (np.random.uniform(0.5, 2.0, (N, V))).astype(np.float32),
        "budg": (np.tile(np.random.uniform(0.1, 0.7, V), (P, 1))).astype(np.float32),
        "cap": (np.tile(np.random.uniform(1.0, 2.5, V), (P, 1))).astype(np.float32),
        "offs": striped(np.random.permutation(T)[:S]),
    }


def reference(x_words, x_scales, w1, w2, mult, budg, cap, offs):
    xq = unpack_weight(x_words, x_scales)[:, unstriped(offs)]
    yv = mxq(f64(w1), 0, "e4m3").T @ xq
    val = np.log(np.exp(yv) + 1.0) + 0.2
    bid = val / (np.repeat(f64(mult), D, axis=1) + 0.3)
    yp = mxq(f64(w2), 0, "e4m3").T @ xq
    pri = np.log(np.exp(yp) + 1.0)
    win = sigmoid(4.0 * (bid - pri))
    pay = win * pri
    spend = pay.reshape(len(pay), -1, D).mean(axis=2)
    mnew = f64(mult) * (np.exp(0.8 * (spend - f64(budg)[:1])))
    return np.minimum(mnew, f64(cap)[:1])

@@ -1,0 +1,167 @@
+from contextlib import ExitStack
+
+import concourse.mybir as mybir
+
+K, T, S, D, N, V = 512, 4096, 1024, 8, 128, 128
+FLOPS = 2 * 2 * K * N * S
+
+F32 = mybir.dt.float32
+BF16 = mybir.dt.bfloat16
+I32 = mybir.dt.int32
+U32 = mybir.dt.uint32
+U16 = mybir.dt.uint16
+U8 = mybir.dt.uint8
+FP8X4 = mybir.dt.float8_e4m3fn_x4
+ALU = mybir.AluOpType
+ACT = mybir.ActivationFunctionType
+AX = mybir.AxisListType
+
+P = 128
+PACK = 4
+HALF = S // 2
+CHUNK = 256
+CHUNKS = S // CHUNK
+GROUPS = CHUNK // D
+TINY = 2.0 ** -60
+BIG = 2.0 ** 100
+
+
+def tile_picked_ypacng_mult_p_kernel(
+    tc, x_words, x_scales, w1, w2, mult, budg, cap, offs, out
+):
+    nc = tc.nc
+    with ExitStack() as ctx:
+        keep = ctx.enter_context(tc.tile_pool(name="keep", bufs=1))
+        psum = ctx.enter_context(tc.psum_pool(name="psum", bufs=1))
+
+        offsets = keep.tile([P, S // 16], U16, name="offsets")
+        nc.sync.dma_start(offsets[:], offs)
+
+        scale_table = keep.tile([P, T], U8, name="scale_table", tag="scale_slot", align_bytes=64)
+        nc.vector.memset(scale_table[:].bitcast(I32), 0)
+        for q in range(4):
+            nc.scalar.dma_start(
+                out=scale_table[32 * q : 32 * q + 4, :].bitcast(I32),
+                in_=x_scales[0, 4 * q : 4 * q + 4, :].bitcast(I32),
+            )
+
+        w_raw = keep.tile([P, 2, PACK, N], F32, name="w_raw", tag="stage")
+        for i, w in enumerate((w1, w2)):
+            nc.sync.dma_start(out=w_raw[:, i], in_=w.rearrange("(p j) n -> p j n", j=PACK))
+
+        zero = keep.tile([P, 1], F32, name="zero", tag="word_slot", align_bytes=64)
+        tiny = keep.tile([P, 1], F32, name="tiny")
+        nc.vector.memset(zero[:], 0.0)
+        nc.vector.tensor_scalar_add(tiny[:], zero[:], TINY)
+        word_table = keep.tile([P, T], U32, name="word_table", tag="word_slot", align_bytes=64)
+        nc.sync.dma_start(
+            out=word_table[:].bitcast(I32),
+            in_=x_words[0].rearrange("p n t -> p (n t)").bitcast(I32),
+        )
+
+        warm = keep.tile([P, 1], F32, name="warm")
+        nc.scalar.activation(warm[:], tiny[:], ACT.Sigmoid)
+
+        w_codes = keep.tile([P, 2 * N], U32, name="w_codes", align_bytes=64)
+        w_scales = keep.tile([P, 2 * N], U8, name="w_scales", align_bytes=64)
+        w_bf = keep.tile([P, 2, N, PACK], BF16, name="w_bf", align_bytes=64)
+        for i in range(2):
+            nc.scalar.copy(out=w_bf[:, i], in_=w_raw[:, i].rearrange("p j n -> p n j"))
+
+        picked_scales = [keep.tile([P, HALF], U8, name=f"picked_scales{h}", align_bytes=64) for h in range(2)]
+        cols = HALF // 16
+        for h in range(2):
+            nc.vector.tensor_copy(
+                picked_scales[h][:], scale_table[:].indirect(offsets[:, h * cols : (h + 1) * cols])
+            )
+        nc.vector.quantize_mx(
+            out=w_codes[:].bitcast(FP8X4),
+            scales=w_scales[:],
+            in_=w_bf[:].rearrange("p i n j -> p (i n j)"),
+        )
+        picked_words = keep.tile([P, S], U32, name="picked_words", tag="scale_slot", align_bytes=64)
+        for h in range(2):
+            nc.vector.tensor_copy(
+                picked_words[:, h * HALF : (h + 1) * HALF], word_table[:].indirect(offsets[:, h * cols : (h + 1) * cols])
+            )
+
+        small = keep.tile([P, 3, V], F32, name="small", tag="stage")
+        for i, src in enumerate((mult, budg, cap)):
+            nc.sync.dma_start(out=small[:, i, :], in_=src)
+        mult_sb, budg_sb, cap_sb = small[:, 0, :], small[:, 1, :], small[:, 2, :]
+
+        y = [psum.tile([P, 2, CHUNK], F32, name=f"y{c}") for c in range(CHUNKS)]
+        for c in range(CHUNKS):
+            h, c0 = divmod(c * CHUNK, HALF)
+            for i in range(2):
+                nc.tensor.matmul_mx(
+                    out=y[c][:, i, :],
+                    lhsT=w_codes[:, i * N : (i + 1) * N].bitcast(FP8X4),
+                    lhsT_scale=w_scales[:, i * N : (i + 1) * N],
+                    rhs=picked_words[:, c * CHUNK : (c + 1) * CHUNK].bitcast(FP8X4),
+                    rhs_scale=picked_scales[h][:, c0 : c0 + CHUNK],
+                    start=True,
+                    stop=True,
+                )
+
+        sig = [keep.tile([P, 2, CHUNK], F32, name=f"sig{c}") for c in range(CHUNKS)]
+        for c in range(CHUNKS):
+            nc.scalar.activation(sig[c][:], y[c][:], ACT.Sigmoid, scale=-1.0)
+
+        shifted = keep.tile([P, V], F32, name="shifted")
+        recip = keep.tile([P, V], F32, name="recip")
+        nc.vector.tensor_scalar_add(shifted[:], mult_sb, 0.3)
+        nc.vector.reciprocal(recip[:], shifted[:])
+
+        pay = [keep.tile([P, GROUPS, 12], F32, name=f"pay{c}") for c in range(CHUNKS)]
+        for c in range(CHUNKS):
+            nc.vector.tensor_scalar_mul(pay[c][:, :, D], budg_sb[:, c * GROUPS : (c + 1) * GROUPS], -2.0 * D)
+
+        logsig = [keep.tile([P, 2, CHUNK], F32, name=f"logsig{c}") for c in range(CHUNKS)]
+        for c in range(CHUNKS):
+            nc.scalar.activation(logsig[c][:], sig[c][:], ACT.Ln, bias=tiny[:])
+
+        soft = [keep.tile([P, 2, CHUNK], F32, name=f"soft{c}") for c in range(CHUNKS)]
+        bid = [keep.tile([P, GROUPS, D], F32, name=f"bid{c}") for c in range(CHUNKS)]
+        margin = [keep.tile([P, CHUNK], F32, name=f"margin{c}") for c in range(CHUNKS)]
+        for c in range(CHUNKS):
+            vs = slice(c * GROUPS, (c + 1) * GROUPS)
+            nc.vector.scalar_tensor_tensor(
+                soft[c][:], logsig[c][:], -1.0, y[c][:], ALU.mult, ALU.max
+            )
+            nc.vector.scalar_tensor_tensor(
+                bid[c][:],
+                soft[c][:, 0, :].rearrange("p (v d) -> p v d", d=D),
+                0.2,
+                recip[:, vs].unsqueeze(2).to_broadcast([P, GROUPS, D]),
+                ALU.add,
+                ALU.mult,
+            )
+            nc.vector.tensor_tensor(
+                margin[c][:], bid[c][:].rearrange("p v d -> p (v d)"), soft[c][:, 1, :], ALU.subtract
+            )
+
+        th = [keep.tile([P, CHUNK], F32, name=f"th{c}") for c in range(CHUNKS)]
+        for c in range(CHUNKS):
+            nc.scalar.activation(th[c][:], margin[c][:], ACT.Tanh, scale=2.0)
+
+        total = keep.tile([P, V], F32, name="total")
+        for c in range(CHUNKS):
+            vs = slice(c * GROUPS, (c + 1) * GROUPS)
+            nc.vector.scalar_tensor_tensor(
+                pay[c][:, :, 0:D],
+                th[c][:].rearrange("p (v d) -> p v d", d=D),
+                1.0,
+                soft[c][:, 1, :].rearrange("p (v d) -> p v d", d=D),
+                ALU.add,
+                ALU.mult,
+            )
+            nc.vector.tensor_reduce(total[:, vs], pay[c][:, :, 0 : D + 1], AX.X, ALU.add)
+
+        grow = keep.tile([P, V], F32, name="grow")
+        mnew = keep.tile([P, V], F32, name="mnew")
+        result = keep.tile([P, V], F32, name="result")
+        nc.scalar.activation(grow[:], total[:], ACT.Exp, scale=0.8 / (2 * D))
+        nc.vector.scalar_tensor_tensor(mnew[:], grow[:], BIG, mult_sb, ALU.min, ALU.mult)
+        nc.vector.tensor_tensor(result[:], mnew[:], cap_sb, ALU.min)
+        nc.sync.dma_start(out=out, in_=result[:])

@@ -40,7 +40,7 @@ def tile_picked_ypacng_mult_p_kernel(
         scale_table = keep.tile([P, T], U8, name="scale_table", tag="scale_slot", align_bytes=64)
         nc.vector.memset(scale_table[:].bitcast(I32), 0)
         for q in range(4):
-            nc.scalar.dma_start(
+            nc.sync.dma_start(
                 out=scale_table[32 * q : 32 * q + 4, :].bitcast(I32),
                 in_=x_scales[0, 4 * q : 4 * q + 4, :].bitcast(I32),
             )
@@ -124,39 +124,45 @@ def tile_picked_ypacng_mult_p_kernel(
         soft = [keep.tile([P, 2, CHUNK], F32, name=f"soft{c}") for c in range(CHUNKS)]
         bid = [keep.tile([P, GROUPS, D], F32, name=f"bid{c}") for c in range(CHUNKS)]
         margin = [keep.tile([P, CHUNK], F32, name=f"margin{c}") for c in range(CHUNKS)]
-        for c in range(CHUNKS):
-            vs = slice(c * GROUPS, (c + 1) * GROUPS)
-            nc.vector.scalar_tensor_tensor(
-                soft[c][:], logsig[c][:], -1.0, y[c][:], ALU.mult, ALU.max
-            )
-            nc.vector.scalar_tensor_tensor(
-                bid[c][:],
-                soft[c][:, 0, :].rearrange("p (v d) -> p v d", d=D),
-                0.2,
-                recip[:, vs].unsqueeze(2).to_broadcast([P, GROUPS, D]),
-                ALU.add,
-                ALU.mult,
-            )
-            nc.vector.tensor_tensor(
-                margin[c][:], bid[c][:].rearrange("p v d -> p (v d)"), soft[c][:, 1, :], ALU.subtract
-            )
-
         th = [keep.tile([P, CHUNK], F32, name=f"th{c}") for c in range(CHUNKS)]
-        for c in range(CHUNKS):
+        total = keep.tile([P, V], F32, name="total")
+
+        def by_group(ap):
+            return ap.rearrange("p (v d) -> p v d", d=D)
+
+        def softplus(c):
+            nc.vector.scalar_tensor_tensor(soft[c][:], logsig[c][:], -1.0, y[c][:], ALU.mult, ALU.max)
+
+        def make_bid(c):
+            r = recip[:, c * GROUPS : (c + 1) * GROUPS].unsqueeze(2).to_broadcast([P, GROUPS, D])
+            nc.vector.scalar_tensor_tensor(bid[c][:], by_group(soft[c][:, 0, :]), 0.2, r, ALU.add, ALU.mult)
+
+        def make_margin(c):
+            nc.vector.tensor_tensor(by_group(margin[c][:]), bid[c][:], by_group(soft[c][:, 1, :]), ALU.subtract)
+
+        def make_win(c):
             nc.scalar.activation(th[c][:], margin[c][:], ACT.Tanh, scale=2.0)
 
-        total = keep.tile([P, V], F32, name="total")
-        for c in range(CHUNKS):
-            vs = slice(c * GROUPS, (c + 1) * GROUPS)
+        def make_pay(c):
             nc.vector.scalar_tensor_tensor(
-                pay[c][:, :, 0:D],
-                th[c][:].rearrange("p (v d) -> p v d", d=D),
-                1.0,
-                soft[c][:, 1, :].rearrange("p (v d) -> p v d", d=D),
-                ALU.add,
-                ALU.mult,
+                pay[c][:, :, 0:D], by_group(th[c][:]), 1.0, by_group(soft[c][:, 1, :]), ALU.add, ALU.mult
             )
-            nc.vector.tensor_reduce(total[:, vs], pay[c][:, :, 0 : D + 1], AX.X, ALU.add)
+
+        def sum_pay(c):
+            nc.vector.tensor_reduce(
+                total[:, c * GROUPS : (c + 1) * GROUPS], pay[c][:, :, 0 : D + 1], AX.X, ALU.add
+            )
+
+        for step in range(CHUNKS + 2):
+            for lag, stage in enumerate((softplus, make_bid, make_margin)):
+                if 0 <= step - lag < CHUNKS:
+                    stage(step - lag)
+        for c in range(CHUNKS):
+            make_win(c)
+        for step in range(CHUNKS + 1):
+            for lag, stage in enumerate((make_pay, sum_pay)):
+                if 0 <= step - lag < CHUNKS:
+                    stage(step - lag)
 
         grow = keep.tile([P, V], F32, name="grow")
         mnew = keep.tile([P, V], F32, name="mnew")

@@ -38,75 +38,90 @@ def tile_picked_ypacng_mult_p_kernel(
         nc.sync.dma_start(offsets[:], offs)
 
         scale_table = keep.tile([P, T], U8, name="scale_table", tag="scale_slot", align_bytes=64)
-        nc.vector.memset(scale_table[:].bitcast(I32), 0)
-        for q in range(4):
-            nc.sync.dma_start(
-                out=scale_table[32 * q : 32 * q + 4, :].bitcast(I32),
-                in_=x_scales[0, 4 * q : 4 * q + 4, :].bitcast(I32),
-            )
+        nc.sync.dma_start(out=scale_table[P - 16 : P, :].bitcast(I32), in_=x_scales[0].bitcast(I32))
+        nc.vector.memset(scale_table[0 : P - 16, :].bitcast(I32), 0)
 
-        w_raw = keep.tile([P, 2, PACK, N], F32, name="w_raw", tag="stage")
-        for i, w in enumerate((w1, w2)):
-            nc.sync.dma_start(out=w_raw[:, i], in_=w.rearrange("(p j) n -> p j n", j=PACK))
-
-        zero = keep.tile([P, 1], F32, name="zero", tag="word_slot", align_bytes=64)
-        tiny = keep.tile([P, 1], F32, name="tiny")
-        nc.vector.memset(zero[:], 0.0)
-        nc.vector.tensor_scalar_add(tiny[:], zero[:], TINY)
-        word_table = keep.tile([P, T], U32, name="word_table", tag="word_slot", align_bytes=64)
+        w1_raw = keep.tile([P, PACK, N], F32, name="w1_raw")
+        nc.sync.dma_start(out=w1_raw[:], in_=w1.rearrange("(p j) n -> p j n", j=PACK))
+        word_table = keep.tile([P, T], U32, name="word_table", align_bytes=64)
         nc.sync.dma_start(
             out=word_table[:].bitcast(I32),
             in_=x_words[0].rearrange("p n t -> p (n t)").bitcast(I32),
         )
+        w2_raw = keep.tile([P, PACK, N], F32, name="w2_raw")
+        nc.sync.dma_start(out=w2_raw[:], in_=w2.rearrange("(p j) n -> p j n", j=PACK))
+        w_raw = (w1_raw, w2_raw)
 
-        warm = keep.tile([P, 1], F32, name="warm")
-        nc.scalar.activation(warm[:], tiny[:], ACT.Sigmoid)
+        warm = keep.tile([P, 2], F32, name="warm")
+        nc.gpsimd.memset(warm[:, 0:1], 0.0)
+        nc.scalar.activation(warm[:, 1:2], warm[:, 0:1], ACT.Sigmoid)
 
-        w_codes = keep.tile([P, 2 * N], U32, name="w_codes", align_bytes=64)
-        w_scales = keep.tile([P, 2 * N], U8, name="w_scales", align_bytes=64)
-        w_bf = keep.tile([P, 2, N, PACK], BF16, name="w_bf", align_bytes=64)
+        w_codes = [keep.tile([P, N], U32, name=f"w_codes{i}", align_bytes=64) for i in range(2)]
+        w_scales = [keep.tile([P, N], U8, name=f"w_scales{i}", align_bytes=64) for i in range(2)]
+        w_bf = [keep.tile([P, N, PACK], BF16, name=f"w_bf{i}", tag=f"bf_slot{i}", align_bytes=64) for i in range(2)]
         for i in range(2):
-            nc.scalar.copy(out=w_bf[:, i], in_=w_raw[:, i].rearrange("p j n -> p n j"))
+            nc.scalar.copy(out=w_bf[i][:], in_=w_raw[i][:].rearrange("p j n -> p n j"))
 
-        picked_scales = [keep.tile([P, HALF], U8, name=f"picked_scales{h}", align_bytes=64) for h in range(2)]
         cols = HALF // 16
-        for h in range(2):
-            nc.vector.tensor_copy(
-                picked_scales[h][:], scale_table[:].indirect(offsets[:, h * cols : (h + 1) * cols])
-            )
-        nc.vector.quantize_mx(
-            out=w_codes[:].bitcast(FP8X4),
-            scales=w_scales[:],
-            in_=w_bf[:].rearrange("p i n j -> p (i n j)"),
-        )
-        picked_words = keep.tile([P, S], U32, name="picked_words", tag="scale_slot", align_bytes=64)
-        for h in range(2):
-            nc.vector.tensor_copy(
-                picked_words[:, h * HALF : (h + 1) * HALF], word_table[:].indirect(offsets[:, h * cols : (h + 1) * cols])
+        planes = keep.tile([P, S], U8, name="planes", align_bytes=64)
+        nc.vector.memset(planes[:].bitcast(I32), 0)
+        spread = keep.tile([P, S], U8, name="spread", tag="spread_slot", align_bytes=64)
+        nc.vector.tensor_copy(spread[:], scale_table[:].indirect(offsets[:]))
+        for q in range(4):
+            queue = nc.scalar if q < 2 else nc.sync
+            queue.dma_start(
+                out=planes[32 * q : 32 * q + 4, :].bitcast(I32),
+                in_=spread[P - 16 + 4 * q : P - 12 + 4 * q, :].bitcast(I32),
             )
 
-        small = keep.tile([P, 3, V], F32, name="small", tag="stage")
+        def quantize(i):
+            nc.vector.quantize_mx(
+                out=w_codes[i][:].bitcast(FP8X4),
+                scales=w_scales[i][:],
+                in_=w_bf[i][:].rearrange("p n j -> p (n j)"),
+            )
+
+        picked_words = []
+        for h, slot in enumerate(("scale_slot", "bf_slot1")):
+            if h == 0:
+                quantize(0)
+            else:
+                quantize(1)
+            picked = keep.tile([P, HALF], U32, name=f"picked_words{h}", tag=slot, align_bytes=64)
+            nc.vector.tensor_copy(picked[:], word_table[:].indirect(offsets[:, h * cols : (h + 1) * cols]))
+            picked_words.append(picked)
+
+        small = keep.tile([P, 3, V], F32, name="small", tag="spread_slot", align_bytes=64)
         for i, src in enumerate((mult, budg, cap)):
             nc.sync.dma_start(out=small[:, i, :], in_=src)
         mult_sb, budg_sb, cap_sb = small[:, 0, :], small[:, 1, :], small[:, 2, :]
 
-        y = [psum.tile([P, 2, CHUNK], F32, name=f"y{c}") for c in range(CHUNKS)]
-        for c in range(CHUNKS):
-            h, c0 = divmod(c * CHUNK, HALF)
+        banks = []
+        first = 0
+        for width in (128, 128, 256, 256, 128, 128):
+            banks.append((first, width))
+            first = first + width
+
+        def home(b):
+            c, c0 = divmod(banks[b][0], CHUNK)
+            return c, slice(c0, c0 + banks[b][1])
+
+        y = [psum.tile([P, 2, width], F32, name=f"y{b}") for b, (start, width) in enumerate(banks)]
+        for b, (start, width) in enumerate(banks):
             for i in range(2):
                 nc.tensor.matmul_mx(
-                    out=y[c][:, i, :],
-                    lhsT=w_codes[:, i * N : (i + 1) * N].bitcast(FP8X4),
-                    lhsT_scale=w_scales[:, i * N : (i + 1) * N],
-                    rhs=picked_words[:, c * CHUNK : (c + 1) * CHUNK].bitcast(FP8X4),
-                    rhs_scale=picked_scales[h][:, c0 : c0 + CHUNK],
+                    out=y[b][:, i, :],
+                    lhsT=w_codes[i][:].bitcast(FP8X4),
+                    lhsT_scale=w_scales[i][:],
+                    rhs=picked_words[start // HALF][:, start % HALF : start % HALF + width].bitcast(FP8X4),
+                    rhs_scale=planes[:, start : start + width],
                     start=True,
                     stop=True,
                 )
 
-        sig = [keep.tile([P, 2, CHUNK], F32, name=f"sig{c}") for c in range(CHUNKS)]
-        for c in range(CHUNKS):
-            nc.scalar.activation(sig[c][:], y[c][:], ACT.Sigmoid, scale=-1.0)
+        sig = [keep.tile([P, 2, width], F32, name=f"sig{b}") for b, (start, width) in enumerate(banks)]
+        for b in range(len(banks)):
+            nc.scalar.activation(sig[b][:], y[b][:], ACT.Sigmoid, scale=-1.0)
 
         shifted = keep.tile([P, V], F32, name="shifted")
         recip = keep.tile([P, V], F32, name="recip")
@@ -117,11 +132,11 @@ def tile_picked_ypacng_mult_p_kernel(
         for c in range(CHUNKS):
             nc.vector.tensor_scalar_mul(pay[c][:, :, D], budg_sb[:, c * GROUPS : (c + 1) * GROUPS], -2.0 * D)
 
-        logsig = [keep.tile([P, 2, CHUNK], F32, name=f"logsig{c}") for c in range(CHUNKS)]
-        for c in range(CHUNKS):
-            nc.scalar.activation(logsig[c][:], sig[c][:], ACT.Ln, bias=tiny[:])
+        logsig = [keep.tile([P, 2, width], F32, name=f"logsig{b}") for b, (start, width) in enumerate(banks)]
+        for b in range(len(banks)):
+            nc.scalar.activation(logsig[b][:], sig[b][:], ACT.Ln, bias=TINY)
 
-        soft = [keep.tile([P, 2, CHUNK], F32, name=f"soft{c}") for c in range(CHUNKS)]
+        val = [keep.tile([P, 2, CHUNK], F32, name=f"soft{c}") for c in range(CHUNKS)]
         bid = [keep.tile([P, GROUPS, D], F32, name=f"bid{c}") for c in range(CHUNKS)]
         margin = [keep.tile([P, CHUNK], F32, name=f"margin{c}") for c in range(CHUNKS)]
         th = [keep.tile([P, CHUNK], F32, name=f"th{c}") for c in range(CHUNKS)]
@@ -131,21 +146,37 @@ def tile_picked_ypacng_mult_p_kernel(
             return ap.rearrange("p (v d) -> p v d", d=D)
 
         def softplus(c):
-            nc.vector.scalar_tensor_tensor(soft[c][:], logsig[c][:], -1.0, y[c][:], ALU.mult, ALU.max)
+            for b in range(len(banks)):
+                if home(b)[0] == c:
+                    nc.vector.scalar_tensor_tensor(
+                        val[c][:, :, home(b)[1]], logsig[b][:], -1.0, y[b][:], ALU.mult, ALU.max
+                    )
 
         def make_bid(c):
-            r = recip[:, c * GROUPS : (c + 1) * GROUPS].unsqueeze(2).to_broadcast([P, GROUPS, D])
-            nc.vector.scalar_tensor_tensor(bid[c][:], by_group(soft[c][:, 0, :]), 0.2, r, ALU.add, ALU.mult)
+            parts = 2 if c == 0 else 1
+            g = GROUPS // parts
+            for part in range(parts):
+                v0 = c * GROUPS + part * g
+                r = recip[:, v0 : v0 + g].unsqueeze(2).to_broadcast([P, g, D])
+                nc.vector.scalar_tensor_tensor(
+                    bid[c][:, part * g : (part + 1) * g, :],
+                    by_group(val[c][:, 0, part * g * D : (part + 1) * g * D]),
+                    0.2,
+                    r,
+                    ALU.add,
+                    ALU.mult,
+                )
 
         def make_margin(c):
-            nc.vector.tensor_tensor(by_group(margin[c][:]), bid[c][:], by_group(soft[c][:, 1, :]), ALU.subtract)
+            engine = nc.gpsimd if c < 2 else nc.vector
+            engine.tensor_tensor(by_group(margin[c][:]), bid[c][:], by_group(val[c][:, 1, :]), ALU.subtract)
 
         def make_win(c):
             nc.scalar.activation(th[c][:], margin[c][:], ACT.Tanh, scale=2.0)
 
         def make_pay(c):
             nc.vector.scalar_tensor_tensor(
-                pay[c][:, :, 0:D], by_group(th[c][:]), 1.0, by_group(soft[c][:, 1, :]), ALU.add, ALU.mult
+                pay[c][:, :, 0:D], by_group(th[c][:]), 1.0, by_group(val[c][:, 1, :]), ALU.add, ALU.mult
             )
 
         def sum_pay(c):
@@ -164,10 +195,12 @@ def tile_picked_ypacng_mult_p_kernel(
                 if 0 <= step - lag < CHUNKS:
                     stage(step - lag)
 
-        grow = keep.tile([P, V], F32, name="grow")
-        mnew = keep.tile([P, V], F32, name="mnew")
-        result = keep.tile([P, V], F32, name="result")
-        nc.scalar.activation(grow[:], total[:], ACT.Exp, scale=0.8 / (2 * D))
-        nc.vector.scalar_tensor_tensor(mnew[:], grow[:], BIG, mult_sb, ALU.min, ALU.mult)
-        nc.vector.tensor_tensor(result[:], mnew[:], cap_sb, ALU.min)
-        nc.sync.dma_start(out=out, in_=result[:])
+        for part, vs in enumerate((slice(0, V - GROUPS), slice(V - GROUPS, V))):
+            width = vs.stop - vs.start
+            grow = keep.tile([P, width], F32, name=f"grow{part}")
+            mnew = keep.tile([P, width], F32, name=f"mnew{part}")
+            result = keep.tile([P, width], F32, name=f"result{part}")
+            nc.scalar.activation(grow[:], total[:, vs], ACT.Exp, scale=0.8 / (2 * D))
+            nc.vector.scalar_tensor_tensor(mnew[:], grow[:], BIG, mult_sb[:, vs], ALU.min, ALU.mult)
+            nc.vector.tensor_tensor(result[:], mnew[:], cap_sb[:, vs], ALU.min)
+            nc.sync.dma_start(out=out[:, vs], in_=result[:])

@@ -41,13 +41,13 @@ def tile_picked_ypacng_mult_p_kernel(
         nc.sync.dma_start(out=scale_table[P - 16 : P, :].bitcast(I32), in_=x_scales[0].bitcast(I32))
         nc.vector.memset(scale_table[0 : P - 16, :].bitcast(I32), 0)
 
-        w1_raw = keep.tile([P, PACK, N], F32, name="w1_raw")
-        nc.sync.dma_start(out=w1_raw[:], in_=w1.rearrange("(p j) n -> p j n", j=PACK))
         word_table = keep.tile([P, T], U32, name="word_table", align_bytes=64)
         nc.sync.dma_start(
             out=word_table[:].bitcast(I32),
             in_=x_words[0].rearrange("p n t -> p (n t)").bitcast(I32),
         )
+        w1_raw = keep.tile([P, PACK, N], F32, name="w1_raw")
+        nc.sync.dma_start(out=w1_raw[:], in_=w1.rearrange("(p j) n -> p j n", j=PACK))
         w2_raw = keep.tile([P, PACK, N], F32, name="w2_raw")
         nc.sync.dma_start(out=w2_raw[:], in_=w2.rearrange("(p j) n -> p j n", j=PACK))
         w_raw = (w1_raw, w2_raw)
@@ -59,8 +59,7 @@ def tile_picked_ypacng_mult_p_kernel(
         w_codes = [keep.tile([P, N], U32, name=f"w_codes{i}", align_bytes=64) for i in range(2)]
         w_scales = [keep.tile([P, N], U8, name=f"w_scales{i}", align_bytes=64) for i in range(2)]
         w_bf = [keep.tile([P, N, PACK], BF16, name=f"w_bf{i}", tag=f"bf_slot{i}", align_bytes=64) for i in range(2)]
-        for i in range(2):
-            nc.scalar.copy(out=w_bf[i][:], in_=w_raw[i][:].rearrange("p j n -> p n j"))
+        nc.scalar.copy(out=w_bf[0][:], in_=w_raw[0][:].rearrange("p j n -> p n j"))
 
         cols = HALF // 16
         planes = keep.tile([P, S], U8, name="planes", align_bytes=64)
@@ -83,9 +82,9 @@ def tile_picked_ypacng_mult_p_kernel(
 
         picked_words = []
         for h, slot in enumerate(("scale_slot", "bf_slot1")):
-            if h == 0:
+            if h == 1:
+                nc.vector.tensor_copy(out=w_bf[1][:], in_=w_raw[1][:].rearrange("p j n -> p n j"))
                 quantize(0)
-            else:
                 quantize(1)
             picked = keep.tile([P, HALF], U32, name=f"picked_words{h}", tag=slot, align_bytes=64)
             nc.vector.tensor_copy(picked[:], word_table[:].indirect(offsets[:, h * cols : (h + 1) * cols]))
@@ -98,7 +97,7 @@ def tile_picked_ypacng_mult_p_kernel(
 
         banks = []
         first = 0
-        for width in (128, 128, 256, 256, 128, 128):
+        for width in (128, 128, 256, 128, 128, 256):
             banks.append((first, width))
             first = first + width
 

from contextlib import ExitStack

import concourse.mybir as mybir

K, T, S, D, N, V = 512, 4096, 1024, 8, 128, 128
FLOPS = 2 * 2 * K * N * S

F32 = mybir.dt.float32
BF16 = mybir.dt.bfloat16
I32 = mybir.dt.int32
U32 = mybir.dt.uint32
U16 = mybir.dt.uint16
U8 = mybir.dt.uint8
FP8X4 = mybir.dt.float8_e4m3fn_x4
ALU = mybir.AluOpType
ACT = mybir.ActivationFunctionType
AX = mybir.AxisListType

P = 128
PACK = 4
HALF = S // 2
CHUNK = 256
CHUNKS = S // CHUNK
GROUPS = CHUNK // D
TINY = 2.0 ** -60
BIG = 2.0 ** 100


def tile_picked_ypacng_mult_p_kernel(
    tc, x_words, x_scales, w1, w2, mult, budg, cap, offs, out
):
    nc = tc.nc
    with ExitStack() as ctx:
        keep = ctx.enter_context(tc.tile_pool(name="keep", bufs=1))
        psum = ctx.enter_context(tc.psum_pool(name="psum", bufs=1))

        offsets = keep.tile([P, S // 16], U16, name="offsets")
        nc.sync.dma_start(offsets[:], offs)

        scale_table = keep.tile([P, T], U8, name="scale_table", tag="scale_slot", align_bytes=64)
        nc.sync.dma_start(out=scale_table[P - 16 : P, :].bitcast(I32), in_=x_scales[0].bitcast(I32))
        nc.vector.memset(scale_table[0 : P - 16, :].bitcast(I32), 0)

        word_table = keep.tile([P, T], U32, name="word_table", align_bytes=64)
        nc.sync.dma_start(
            out=word_table[:].bitcast(I32),
            in_=x_words[0].rearrange("p n t -> p (n t)").bitcast(I32),
        )
        w1_raw = keep.tile([P, PACK, N], F32, name="w1_raw")
        nc.sync.dma_start(out=w1_raw[:], in_=w1.rearrange("(p j) n -> p j n", j=PACK))
        w2_raw = keep.tile([P, PACK, N], F32, name="w2_raw")
        nc.sync.dma_start(out=w2_raw[:], in_=w2.rearrange("(p j) n -> p j n", j=PACK))
        w_raw = (w1_raw, w2_raw)

        warm = keep.tile([P, 2], F32, name="warm")
        nc.gpsimd.memset(warm[:, 0:1], 0.0)
        nc.scalar.activation(warm[:, 1:2], warm[:, 0:1], ACT.Sigmoid)

        w_codes = [keep.tile([P, N], U32, name=f"w_codes{i}", align_bytes=64) for i in range(2)]
        w_scales = [keep.tile([P, N], U8, name=f"w_scales{i}", align_bytes=64) for i in range(2)]
        w_bf = [keep.tile([P, N, PACK], BF16, name=f"w_bf{i}", tag=f"bf_slot{i}", align_bytes=64) for i in range(2)]
        nc.scalar.copy(out=w_bf[0][:], in_=w_raw[0][:].rearrange("p j n -> p n j"))

        cols = HALF // 16
        planes = keep.tile([P, S], U8, name="planes", align_bytes=64)
        nc.vector.memset(planes[:].bitcast(I32), 0)
        spread = keep.tile([P, S], U8, name="spread", tag="spread_slot", align_bytes=64)
        nc.vector.tensor_copy(spread[:], scale_table[:].indirect(offsets[:]))
        for q in range(4):
            queue = nc.scalar if q < 2 else nc.sync
            queue.dma_start(
                out=planes[32 * q : 32 * q + 4, :].bitcast(I32),
                in_=spread[P - 16 + 4 * q : P - 12 + 4 * q, :].bitcast(I32),
            )

        def quantize(i):
            nc.vector.quantize_mx(
                out=w_codes[i][:].bitcast(FP8X4),
                scales=w_scales[i][:],
                in_=w_bf[i][:].rearrange("p n j -> p (n j)"),
            )

        picked_words = []
        for h, slot in enumerate(("scale_slot", "bf_slot1")):
            if h == 1:
                nc.vector.tensor_copy(out=w_bf[1][:], in_=w_raw[1][:].rearrange("p j n -> p n j"))
                quantize(0)
                quantize(1)
            picked = keep.tile([P, HALF], U32, name=f"picked_words{h}", tag=slot, align_bytes=64)
            nc.vector.tensor_copy(picked[:], word_table[:].indirect(offsets[:, h * cols : (h + 1) * cols]))
            picked_words.append(picked)

        small = keep.tile([P, 3, V], F32, name="small", tag="spread_slot", align_bytes=64)
        for i, src in enumerate((mult, budg, cap)):
            nc.sync.dma_start(out=small[:, i, :], in_=src)
        mult_sb, budg_sb, cap_sb = small[:, 0, :], small[:, 1, :], small[:, 2, :]

        banks = []
        first = 0
        for width in (128, 128, 256, 128, 128, 256):
            banks.append((first, width))
            first = first + width

        def home(b):
            c, c0 = divmod(banks[b][0], CHUNK)
            return c, slice(c0, c0 + banks[b][1])

        y = [psum.tile([P, 2, width], F32, name=f"y{b}") for b, (start, width) in enumerate(banks)]
        for b, (start, width) in enumerate(banks):
            for i in range(2):
                nc.tensor.matmul_mx(
                    out=y[b][:, i, :],
                    lhsT=w_codes[i][:].bitcast(FP8X4),
                    lhsT_scale=w_scales[i][:],
                    rhs=picked_words[start // HALF][:, start % HALF : start % HALF + width].bitcast(FP8X4),
                    rhs_scale=planes[:, start : start + width],
                    start=True,
                    stop=True,
                )

        sig = [keep.tile([P, 2, width], F32, name=f"sig{b}") for b, (start, width) in enumerate(banks)]
        for b in range(len(banks)):
            nc.scalar.activation(sig[b][:], y[b][:], ACT.Sigmoid, scale=-1.0)

        shifted = keep.tile([P, V], F32, name="shifted")
        recip = keep.tile([P, V], F32, name="recip")
        nc.vector.tensor_scalar_add(shifted[:], mult_sb, 0.3)
        nc.vector.reciprocal(recip[:], shifted[:])

        pay = [keep.tile([P, GROUPS, 12], F32, name=f"pay{c}") for c in range(CHUNKS)]
        for c in range(CHUNKS):
            nc.vector.tensor_scalar_mul(pay[c][:, :, D], budg_sb[:, c * GROUPS : (c + 1) * GROUPS], -2.0 * D)

        logsig = [keep.tile([P, 2, width], F32, name=f"logsig{b}") for b, (start, width) in enumerate(banks)]
        for b in range(len(banks)):
            nc.scalar.activation(logsig[b][:], sig[b][:], ACT.Ln, bias=TINY)

        val = [keep.tile([P, 2, CHUNK], F32, name=f"soft{c}") for c in range(CHUNKS)]
        bid = [keep.tile([P, GROUPS, D], F32, name=f"bid{c}") for c in range(CHUNKS)]
        margin = [keep.tile([P, CHUNK], F32, name=f"margin{c}") for c in range(CHUNKS)]
        th = [keep.tile([P, CHUNK], F32, name=f"th{c}") for c in range(CHUNKS)]
        total = keep.tile([P, V], F32, name="total")

        def by_group(ap):
            return ap.rearrange("p (v d) -> p v d", d=D)

        def softplus(c):
            for b in range(len(banks)):
                if home(b)[0] == c:
                    nc.vector.scalar_tensor_tensor(
                        val[c][:, :, home(b)[1]], logsig[b][:], -1.0, y[b][:], ALU.mult, ALU.max
                    )

        def make_bid(c):
            parts = 2 if c == 0 else 1
            g = GROUPS // parts
            for part in range(parts):
                v0 = c * GROUPS + part * g
                r = recip[:, v0 : v0 + g].unsqueeze(2).to_broadcast([P, g, D])
                nc.vector.scalar_tensor_tensor(
                    bid[c][:, part * g : (part + 1) * g, :],
                    by_group(val[c][:, 0, part * g * D : (part + 1) * g * D]),
                    0.2,
                    r,
                    ALU.add,
                    ALU.mult,
                )

        def make_margin(c):
            engine = nc.gpsimd if c < 2 else nc.vector
            engine.tensor_tensor(by_group(margin[c][:]), bid[c][:], by_group(val[c][:, 1, :]), ALU.subtract)

        def make_win(c):
            nc.scalar.activation(th[c][:], margin[c][:], ACT.Tanh, scale=2.0)

        def make_pay(c):
            nc.vector.scalar_tensor_tensor(
                pay[c][:, :, 0:D], by_group(th[c][:]), 1.0, by_group(val[c][:, 1, :]), ALU.add, ALU.mult
            )

        def sum_pay(c):
            nc.vector.tensor_reduce(
                total[:, c * GROUPS : (c + 1) * GROUPS], pay[c][:, :, 0 : D + 1], AX.X, ALU.add
            )

        for step in range(CHUNKS + 2):
            for lag, stage in enumerate((softplus, make_bid, make_margin)):
                if 0 <= step - lag < CHUNKS:
                    stage(step - lag)
        for c in range(CHUNKS):
            make_win(c)
        for step in range(CHUNKS + 1):
            for lag, stage in enumerate((make_pay, sum_pay)):
                if 0 <= step - lag < CHUNKS:
                    stage(step - lag)

        for part, vs in enumerate((slice(0, V - GROUPS), slice(V - GROUPS, V))):
            width = vs.stop - vs.start
            grow = keep.tile([P, width], F32, name=f"grow{part}")
            mnew = keep.tile([P, width], F32, name=f"mnew{part}")
            result = keep.tile([P, width], F32, name=f"result{part}")
            nc.scalar.activation(grow[:], total[:, vs], ACT.Exp, scale=0.8 / (2 * D))
            nc.vector.scalar_tensor_tensor(mnew[:], grow[:], BIG, mult_sb[:, vs], ALU.min, ALU.mult)
            nc.vector.tensor_tensor(result[:], mnew[:], cap_sb[:, vs], ALU.min)
            nc.sync.dma_start(out=out[:, vs], in_=result[:])
